import numpy as np, ml_dtypes
CORES = [34,162,290,418,42,426]
N = 6
import mx_ref
NC = 128
BF = ml_dtypes.bfloat16
def setup_inputs(rng):
    def f(*shape):
        return mx_ref.flush((rng.standard_normal(shape, dtype=np.float32) * np.exp2(rng.integers(-2, 3, shape[:-1] + (1,)))).astype(BF))
    return {"w": f(N, 128, 512), "x": f(N, 128, N * 4 * NC)}
def setup_inputs_blocks(rng):
    d = setup_inputs(rng)
    for k in ("w", "x"): d[k] = mx_ref.spread(d[k], rng, 2)
    return d
def setup_inputs_wide(rng):
    d = setup_inputs(rng)
    for k in ("w", "x"): d[k] = mx_ref.flush((d[k].astype(np.float32) * np.exp2(rng.integers(-8, 9, (N, 1, 1))).astype(np.float32)).astype(BF))
    return d
def setup_inputs_zeros(rng):
    d = setup_inputs(rng); v = d["x"].reshape(N, 128, -1, 4).copy()
    v[np.broadcast_to((rng.random((N, 1, v.shape[2], 1)) < 0.33), v.shape)] = 0
    d["x"] = v.reshape(d["x"].shape)
    return d
def reference(w, x):
    QW = [mx_ref.quantize(w[j]) for j in range(N)]
    y = np.zeros((N, 128, NC), np.float32)
    for r in range(N):
        for j in range(N):
            p = mx_ref.matmul(QW[j], mx_ref.quantize(x[j][:, 4 * NC * r:4 * NC * r + 4 * NC]))
            y[r] = p if j == 0 else y[r] + p
    return {"y": y}

@@ -1,0 +1,160 @@
+from concourse.bass import DstId, RemoteDMATransfer
+from concourse.mybir import dt
+
+N = 6
+TW = 128
+TB = 4 * TW
+SLOT = 4
+OWN = N
+KINDS = ("s", "c")
+
+SCRATCH = {
+    "wt": ("sbuf", [128, TB], "bfloat16"),
+    "xt": ("sbuf", [128, N * TB], "bfloat16"),
+    "qc": ("sbuf", [128, (N + 1) * SLOT * TW], "float8_e4m3fn_x4"),
+    "qs": ("sbuf", [128, (N + 1) * SLOT * TW], "uint8"),
+    "acc": ("psum", [128, 512], "float32"),
+    "yt": ("sbuf", [128, TW], "float32"),
+}
+SEMAPHORES = (["ldw"] + ["ldx%d" % k for k in range(N)] + ["qb", "qn", "qo", "sent", "mm", "cp", "st"]
+              + ["arr%s%d" % (kind, j) for kind in KINDS for j in range(N)])
+
+
+def _plan(cores, topo):
+    plan = []
+    for j, cj in enumerate(cores):
+        rack = topo.rack(topo.host(cj))
+        near = [r for r, c in enumerate(cores) if r != j and topo.rack(topo.host(c)) == rack]
+        far = [r for r, c in enumerate(cores) if topo.rack(topo.host(c)) != rack]
+        p = [r for r in far if topo.may_write(cj, cores[r]) and topo.chip(cores[r]) == topo.chip(cj)][0]
+        a, b = [r for r in far if r != p]
+        plan.append({"p": p, "a": a, "b": b, "c": near[0], "d": near[1]})
+    return plan
+
+
+def _runs(tiles):
+    out = []
+    for t in sorted(tiles):
+        if out and out[-1][0] + out[-1][1] == t:
+            out[-1] = (out[-1][0], out[-1][1] + 1)
+        else:
+            out.append((t, 1))
+    return out
+
+
+def _engines(mask):
+    return [1 << k for k in range(16) if mask >> k & 1]
+
+
+def _join(bits):
+    m = 0
+    for b in bits:
+        m |= b
+    return m
+
+
+def _cols(slot, pos, tiles=1):
+    lo = (slot * SLOT + pos) * TW
+    return lo, lo + tiles * TW
+
+
+def rank_program(g, core, T, topo):
+    me = T.rank_of(core)
+    if me is None:
+        return
+    cores = list(T.cores)
+    plan = _plan(cores, topo)
+    P = plan[me]
+    p, a, b, c, d = P["p"], P["a"], P["b"], P["c"], P["d"]
+    sem = T.sem
+
+    def view(kind, lo, hi):
+        return T.qc[:, lo:hi].bitcast(dt.uint8) if kind == "c" else T.qs[:, lo:hi]
+
+    loads = _runs([p, a, b]) + _runs([c, d, me])
+    where = {}
+    g.sync.dma_start(T.wt[:], T.w[:]).then_inc(sem.ldw, 16)
+    queues = [g.scalar, g.sync]
+    for k, (first, count) in enumerate(loads):
+        queues[k % 2].dma_start(T.xt[:, first * TB:(first + count) * TB],
+                                T.x[:, first * TB:(first + count) * TB]).then_inc(sem["ldx%d" % k], 16)
+        for t in range(first, first + count):
+            where[t] = k
+
+    waited = set()
+
+    def quant(tile, slot, pos, done):
+        lo, hi = _cols(slot, pos)
+        if tile is None:
+            if "w" not in waited:
+                g.vector.wait_ge(sem.ldw, 16)
+                waited.add("w")
+            src = T.wt[:]
+        else:
+            if where[tile] not in waited:
+                g.vector.wait_ge(sem["ldx%d" % where[tile]], 16)
+                waited.add(where[tile])
+            src = T.xt[:, tile * TB:(tile + 1) * TB]
+        g.vector.quantize_mx(T.qc[:, lo:hi], T.qs[:, lo:hi], src).then_inc(done, 1)
+
+    quant(None, me, 2, sem.qb)
+    for tile in sorted([p, a, b], key=lambda t: where[t]):
+        quant(tile, me, {p: 0, a: 1, b: 3}[tile], sem.qb)
+    quant(None, OWN, 1, sem.qn)
+    for tile in sorted([c, d], key=lambda t: where[t]):
+        quant(tile, OWN, {c: 0, d: 2}[tile], sem.qn)
+    quant(me, OWN, 3, sem.qo)
+
+    sent = [0]
+
+    def pair(kind, src_slot, src_pos, origin, dst_ranks):
+        trs = []
+        for k, r in enumerate(dst_ranks):
+            eng = _engines(topo.mask(core, cores[r]))
+            half = len(eng) // 2
+            rid, pid = topo.addr(cores[r], core)
+            trs.append(RemoteDMATransfer(dst_ids=[DstId(rid=rid, pnc=pid)], dma_engine_mask=_join(eng[k * half:(k + 1) * half]),
+                                         remote_sem=sem["arr%s%d" % (kind, origin)],
+                                         src=view(kind, *_cols(src_slot, src_pos + k, 2)), dst=view(kind, *_cols(origin, 1 + k, 2))))
+            sent[0] += half
+        g.remote_dma_fused(trs, local_sem=sem.sent)
+
+    g.wait_ge(sem.qb, 4)
+    rid, pid = topo.addr(cores[p], core)
+    full = topo.mask(core, cores[p])
+    lo, hi = _cols(me, 0, SLOT)
+    for kind in KINDS:
+        g.remote_dma(view(kind, lo, hi), view(kind, lo, hi), sem["arr%s%d" % (kind, me)], sem.sent, pid, rid, full)
+        sent[0] += len(_engines(full))
+    g.wait_ge(sem.qn, 3)
+    for kind in KINDS:
+        pair(kind, OWN, 0, me, (c, d))
+    for kind in KINDS:
+        g.wait_ge(sem["arr%s%d" % (kind, p)], len(_engines(topo.mask(cores[p], core))))
+        pair(kind, p, 1, p, (plan[p]["a"], plan[p]["b"]))
+
+    def product(w_slot, w_pos, x_slot, x_pos, first, last):
+        wl, wh = _cols(w_slot, w_pos)
+        xl, xh = _cols(x_slot, x_pos)
+        return g.tensor.matmul_mx(T.acc[:, 0:TW], T.qc[:, wl:wh], T.qs[:, wl:wh], T.qc[:, xl:xh], T.qs[:, xl:xh], first, last)
+
+    g.tensor.wait_ge(sem.qn, 3)
+    g.tensor.wait_ge(sem.qo, 1)
+    product(OWN, 1, OWN, 3, True, False)
+    order = [p, c, d, plan[c]["p"], plan[d]["p"]]
+    for k, j in enumerate(order):
+        Q = plan[j]
+        sender = j if (me == Q["p"] or me in (Q["c"], Q["d"])) else Q["p"]
+        eng = len(_engines(topo.mask(cores[sender], core)))
+        for kind in KINDS:
+            g.tensor.wait_ge(sem["arr%s%d" % (kind, j)], eng if me == Q["p"] else eng // 2)
+        pos = 0 if me == Q["p"] else (1 if me in (Q["a"], Q["c"]) else 3)
+        ins = product(j, 2, j, pos, False, k == len(order) - 1)
+    ins.then_inc(sem.mm, 1)
+
+    g.vector.wait_ge(sem.mm, 1)
+    g.vector.tensor_copy(T.yt[:], T.acc[:, 0:TW]).then_inc(sem.cp, 1)
+    g.sync.wait_ge(sem.cp, 1)
+    g.sync.dma_start(T.y[:], T.yt[:]).then_inc(sem.st, 16)
+    g.sync.wait_ge(sem.st, 16)
+    g.wait_ge(sem.sent, sent[0])

@@ -16,8 +16,8 @@ SCRATCH = {
     "acc": ("psum", [128, 512], "float32"),
     "yt": ("sbuf", [128, TW], "float32"),
 }
-SEMAPHORES = (["ldw"] + ["ldx%d" % k for k in range(N)] + ["qb", "qn", "qo", "sent", "mm", "cp", "st"]
-              + ["arr%s%d" % (kind, j) for kind in KINDS for j in range(N)])
+SEMAPHORES = (["ldw"] + ["ldx%d" % k for k in range(N)] + ["qw", "qb", "qx", "qo", "sent", "mm", "cp", "st"]
+              + ["hw", "hs", "hc", "ps", "pc"] + ["arr%s%d" % (kind, j) for kind in KINDS + ("w",) for j in range(N)])
 
 
 def _plan(cores, topo):
@@ -28,7 +28,13 @@ def _plan(cores, topo):
         far = [r for r, c in enumerate(cores) if topo.rack(topo.host(c)) != rack]
         p = [r for r in far if topo.may_write(cj, cores[r]) and topo.chip(cores[r]) == topo.chip(cj)][0]
         a, b = [r for r in far if r != p]
-        plan.append({"p": p, "a": a, "b": b, "c": near[0], "d": near[1]})
+        chip = [h for h in range(topo.host(cj) * topo.CORES_PER_HOST, (topo.host(cj) + 1) * topo.CORES_PER_HOST)
+                if topo.chip(h) == topo.chip(cj) and h not in cores and topo.die(h) != topo.die(cj)]
+        fit = {r: [h for h in chip if topo.may_write(h, cores[r])] for r in near}
+        helper = {}
+        for r in sorted(near, key=lambda r: len(fit[r])):
+            helper[r] = [h for h in fit[r] if h not in helper.values()][-1]
+        plan.append({"p": p, "a": a, "b": b, "c": near[0], "d": near[1], "h": helper})
     return plan
 
 
@@ -59,19 +65,48 @@ def _cols(slot, pos, tiles=1):
 
 
 def rank_program(g, core, T, topo):
-    me = T.rank_of(core)
-    if me is None:
-        return
     cores = list(T.cores)
     plan = _plan(cores, topo)
-    P = plan[me]
-    p, a, b, c, d = P["p"], P["a"], P["b"], P["c"], P["d"]
     sem = T.sem
+    sent = [0]
 
     def view(kind, lo, hi):
         return T.qc[:, lo:hi].bitcast(dt.uint8) if kind == "c" else T.qs[:, lo:hi]
 
-    loads = _runs([p, a, b]) + _runs([c, d, me])
+    def send(kind, items):
+        trs = []
+        for dst, eng, rsem, s, t in items:
+            rid, pid = topo.addr(dst, core)
+            trs.append(RemoteDMATransfer(dst_ids=[DstId(rid=rid, pnc=pid)], dma_engine_mask=_join(eng), remote_sem=rsem,
+                                         src=view(kind, *s), dst=view(kind, *t)))
+            sent[0] += len(eng)
+        g.remote_dma_fused(trs, local_sem=sem.sent)
+
+    def split(rank):
+        out = _engines(topo.mask(cores[rank], cores[plan[rank]["p"]]))
+        return out, [e for e in _engines(topo.mask(cores[rank], plan[rank]["h"][plan[rank]["c"]])) if e not in out]
+
+    me = T.rank_of(core)
+    if me is None:
+        for j in range(N):
+            for k, r in enumerate((plan[j]["c"], plan[j]["d"])):
+                if plan[j]["h"][r] != core:
+                    continue
+                out, inner = split(j)
+                eng = _engines(topo.mask(core, cores[r]))
+                for kind, letter, count, off, tiles in (("s", "w", (len(out) + len(inner)) // 2, 1, 1),
+                                                        ("s", "s", len(inner) // 2, 2 * k, 1), ("c", "c", len(inner), k, 2)):
+                    g.wait_ge(sem["h" + letter], count)
+                    send(kind, [(cores[r], eng, sem["arr%s%d" % (letter, j)], _cols(OWN, off, tiles), _cols(j, 1 + off, tiles))])
+                g.wait_ge(sem.sent, sent[0])
+        return
+
+    P = plan[me]
+    p, a, b, c, d = P["p"], P["a"], P["b"], P["c"], P["d"]
+    out, inner = split(me)
+    half = len(inner) // 2
+
+    loads = _runs([a, b]) + _runs([p, c, d, me])
     where = {}
     g.sync.dma_start(T.wt[:], T.w[:]).then_inc(sem.ldw, 16)
     queues = [g.scalar, g.sync]
@@ -97,57 +132,53 @@ def rank_program(g, core, T, topo):
             src = T.xt[:, tile * TB:(tile + 1) * TB]
         g.vector.quantize_mx(T.qc[:, lo:hi], T.qs[:, lo:hi], src).then_inc(done, 1)
 
+    quant(None, OWN, 1, sem.qw)
     quant(None, me, 2, sem.qb)
-    for tile in sorted([p, a, b], key=lambda t: where[t]):
-        quant(tile, me, {p: 0, a: 1, b: 3}[tile], sem.qb)
-    quant(None, OWN, 1, sem.qn)
-    for tile in sorted([c, d], key=lambda t: where[t]):
-        quant(tile, OWN, {c: 0, d: 2}[tile], sem.qn)
+    for tile in sorted([a, b], key=lambda t: where[t]):
+        quant(tile, me, {a: 1, b: 3}[tile], sem.qb)
+    for tile in sorted([p, c, d], key=lambda t: where[t]):
+        quant(tile, *{p: (me, 0), c: (OWN, 0), d: (OWN, 2)}[tile], sem.qx)
     quant(me, OWN, 3, sem.qo)
 
-    sent = [0]
-
-    def pair(kind, src_slot, src_pos, origin, dst_ranks):
-        trs = []
-        for k, r in enumerate(dst_ranks):
+    hc, hd = P["h"][c], P["h"][d]
+    w = _cols(OWN, 1)
+    g.wait_ge(sem.qw, 1)
+    send("s", [(hc, out, sem.hw, w, w), (hd, inner, sem.hw, w, w)])
+    send("c", [(hc, inner[:half], sem.hc, w, w), (hd, inner[half:], sem.hc, w, w)])
+    g.wait_ge(sem.qb, 3)
+    for kind in KINDS:
+        send(kind, [(cores[p], out, sem["arr%s%d" % (kind, me)], _cols(me, 1, 3), _cols(me, 1, 3))])
+    g.wait_ge(sem.qx, 3)
+    for kind in KINDS:
+        send(kind, [(cores[p], out, sem["p" + kind], _cols(me, 0), _cols(me, 0)),
+                    (hc, inner[:half], sem["h" + kind], _cols(OWN, 0), _cols(OWN, 0)),
+                    (hd, inner[half:], sem["h" + kind], _cols(OWN, 2), _cols(OWN, 2))])
+    for kind in KINDS:
+        g.wait_ge(sem["arr%s%d" % (kind, p)], len(out))
+        items = []
+        for k, r in enumerate((plan[p]["a"], plan[p]["b"])):
             eng = _engines(topo.mask(core, cores[r]))
-            half = len(eng) // 2
-            rid, pid = topo.addr(cores[r], core)
-            trs.append(RemoteDMATransfer(dst_ids=[DstId(rid=rid, pnc=pid)], dma_engine_mask=_join(eng[k * half:(k + 1) * half]),
-                                         remote_sem=sem["arr%s%d" % (kind, origin)],
-                                         src=view(kind, *_cols(src_slot, src_pos + k, 2)), dst=view(kind, *_cols(origin, 1 + k, 2))))
-            sent[0] += half
-        g.remote_dma_fused(trs, local_sem=sem.sent)
-
-    g.wait_ge(sem.qb, 4)
-    rid, pid = topo.addr(cores[p], core)
-    full = topo.mask(core, cores[p])
-    lo, hi = _cols(me, 0, SLOT)
-    for kind in KINDS:
-        g.remote_dma(view(kind, lo, hi), view(kind, lo, hi), sem["arr%s%d" % (kind, me)], sem.sent, pid, rid, full)
-        sent[0] += len(_engines(full))
-    g.wait_ge(sem.qn, 3)
-    for kind in KINDS:
-        pair(kind, OWN, 0, me, (c, d))
-    for kind in KINDS:
-        g.wait_ge(sem["arr%s%d" % (kind, p)], len(_engines(topo.mask(cores[p], core))))
-        pair(kind, p, 1, p, (plan[p]["a"], plan[p]["b"]))
+            n = len(eng) // 2
+            items.append((cores[r], eng[k * n:(k + 1) * n], sem["arr%s%d" % (kind, p)], _cols(p, 1 + k, 2), _cols(p, 1 + k, 2)))
+        send(kind, items)
 
     def product(w_slot, w_pos, x_slot, x_pos, first, last):
         wl, wh = _cols(w_slot, w_pos)
         xl, xh = _cols(x_slot, x_pos)
         return g.tensor.matmul_mx(T.acc[:, 0:TW], T.qc[:, wl:wh], T.qs[:, wl:wh], T.qc[:, xl:xh], T.qs[:, xl:xh], first, last)
 
-    g.tensor.wait_ge(sem.qn, 3)
+    g.tensor.wait_ge(sem.qw, 1)
     g.tensor.wait_ge(sem.qo, 1)
     product(OWN, 1, OWN, 3, True, False)
     order = [p, c, d, plan[c]["p"], plan[d]["p"]]
     for k, j in enumerate(order):
         Q = plan[j]
-        sender = j if (me == Q["p"] or me in (Q["c"], Q["d"])) else Q["p"]
-        eng = len(_engines(topo.mask(cores[sender], core)))
-        for kind in KINDS:
-            g.tensor.wait_ge(sem["arr%s%d" % (kind, j)], eng if me == Q["p"] else eng // 2)
+        near = me in (Q["c"], Q["d"])
+        for letter in KINDS + (("w",) if near else ()):
+            g.tensor.wait_ge(sem["arr%s%d" % (letter, j)], len(out) if (near or me == Q["p"]) else len(out) // 2)
+        if me == Q["p"]:
+            for kind in KINDS:
+                g.tensor.wait_ge(sem["p" + kind], len(out))
         pos = 0 if me == Q["p"] else (1 if me in (Q["a"], Q["c"]) else 3)
         ins = product(j, 2, j, pos, False, k == len(order) - 1)
     ins.then_inc(sem.mm, 1)

@@ -4,20 +4,20 @@ from concourse.mybir import dt
 N = 6
 TW = 128
 TB = 4 * TW
-SLOT = 4
-OWN = N
+SA, SB, SP, SC, SD = (2 * N + k for k in range(5))
+TILES = 2 * N + 5
 KINDS = ("s", "c")
 
 SCRATCH = {
     "wt": ("sbuf", [128, TB], "bfloat16"),
     "xt": ("sbuf", [128, N * TB], "bfloat16"),
-    "qc": ("sbuf", [128, (N + 1) * SLOT * TW], "float8_e4m3fn_x4"),
-    "qs": ("sbuf", [128, (N + 1) * SLOT * TW], "uint8"),
+    "qc": ("sbuf", [128, TILES * TW], "float8_e4m3fn_x4"),
+    "qs": ("sbuf", [128, TILES * TW], "uint8"),
     "acc": ("psum", [128, 512], "float32"),
     "yt": ("sbuf", [128, TW], "float32"),
 }
-SEMAPHORES = (["ldw"] + ["ldx%d" % k for k in range(N)] + ["qw", "qb", "qx", "qo", "sent", "mm", "cp", "st"]
-              + ["hw", "hs", "hc", "ps", "pc"] + ["arr%s%d" % (kind, j) for kind in KINDS + ("w",) for j in range(N)])
+SEMAPHORES = (["ldw"] + ["ldx%d" % k for k in range(N)] + ["qw", "qb", "qx", "qp", "qo", "go", "sent", "mm", "cp", "st"]
+              + [a + b + k for a in "hr" for b in "wx" for k in KINDS] + ["arr%d" % j for j in range(N)])
 
 
 def _plan(cores, topo):
@@ -29,12 +29,14 @@ def _plan(cores, topo):
         p = [r for r in far if topo.may_write(cj, cores[r]) and topo.chip(cores[r]) == topo.chip(cj)][0]
         a, b = [r for r in far if r != p]
         chip = [h for h in range(topo.host(cj) * topo.CORES_PER_HOST, (topo.host(cj) + 1) * topo.CORES_PER_HOST)
-                if topo.chip(h) == topo.chip(cj) and h not in cores and topo.die(h) != topo.die(cj)]
-        fit = {r: [h for h in chip if topo.may_write(h, cores[r])] for r in near}
+                if topo.chip(h) == topo.chip(cj) and h not in cores]
+        other = [h for h in chip if topo.die(h) != topo.die(cj)]
+        fit = {r: [h for h in other if topo.may_write(h, cores[r])] for r in near}
         helper = {}
         for r in sorted(near, key=lambda r: len(fit[r])):
             helper[r] = [h for h in fit[r] if h not in helper.values()][-1]
-        plan.append({"p": p, "a": a, "b": b, "c": near[0], "d": near[1], "h": helper})
+        relay = [h for h in chip if topo.die(h) == topo.die(cj) and all(topo.may_write(h, cores[r]) for r in near)][-1]
+        plan.append({"p": p, "a": a, "b": b, "c": near[0], "d": near[1], "h": helper, "relay": relay})
     return plan
 
 
@@ -59,9 +61,8 @@ def _join(bits):
     return m
 
 
-def _cols(slot, pos, tiles=1):
-    lo = (slot * SLOT + pos) * TW
-    return lo, lo + tiles * TW
+def _cols(tile, tiles=1):
+    return tile * TW, (tile + tiles) * TW
 
 
 def rank_program(g, core, T, topo):
@@ -82,9 +83,15 @@ def rank_program(g, core, T, topo):
             sent[0] += len(eng)
         g.remote_dma_fused(trs, local_sem=sem.sent)
 
-    def split(rank):
-        out = _engines(topo.mask(cores[rank], cores[plan[rank]["p"]]))
-        return out, [e for e in _engines(topo.mask(cores[rank], plan[rank]["h"][plan[rank]["c"]])) if e not in out]
+    def split(src, off, on):
+        out = _engines(topo.mask(src, off))
+        return out, [e for e in _engines(topo.mask(src, on)) if e not in out]
+
+    def rank_split(j):
+        return split(cores[j], plan[plan[j]["p"]]["relay"], plan[j]["h"][plan[j]["c"]])
+
+    def relay_split(q):
+        return split(plan[q]["relay"], cores[plan[q]["c"]], cores[q])
 
     me = T.rank_of(core)
     if me is None:
@@ -92,38 +99,57 @@ def rank_program(g, core, T, topo):
             for k, r in enumerate((plan[j]["c"], plan[j]["d"])):
                 if plan[j]["h"][r] != core:
                     continue
-                out, inner = split(j)
+                count = len(rank_split(j)[1]) // 2
                 eng = _engines(topo.mask(core, cores[r]))
-                for kind, letter, count, off, tiles in (("s", "w", (len(out) + len(inner)) // 2, 1, 1),
-                                                        ("s", "s", len(inner) // 2, 2 * k, 1), ("c", "c", len(inner), k, 2)):
-                    g.wait_ge(sem["h" + letter], count)
-                    send(kind, [(cores[r], eng, sem["arr%s%d" % (letter, j)], _cols(OWN, off, tiles), _cols(j, 1 + off, tiles))])
+                for what, src, dst in (("w", 2 * j, 2 * j), ("x", SC + k, 2 * j + 1)):
+                    for kind in KINDS:
+                        g.wait_ge(sem["h" + what + kind], count)
+                        send(kind, [(cores[r], eng, sem["arr%d" % j], _cols(src), _cols(dst))])
                 g.wait_ge(sem.sent, sent[0])
+            q = plan[j]["p"]
+            if plan[q]["relay"] != core:
+                continue
+            count = len(rank_split(j)[0])
+            out, inner = relay_split(q)
+            n = len(out) // 2
+            a, b = plan[j]["a"], plan[j]["b"]
+            for kind in KINDS:
+                g.wait_ge(sem["rw" + kind], count)
+                send(kind, [(cores[a], out[:n], sem["arr%d" % j], _cols(2 * j), _cols(2 * j)),
+                            (cores[b], out[n:], sem["arr%d" % j], _cols(2 * j), _cols(2 * j)),
+                            (cores[q], inner, sem["arr%d" % j], _cols(2 * j), _cols(2 * j))])
+            for kind in KINDS:
+                g.wait_ge(sem["rx" + kind], count)
+                send(kind, [(cores[a], out[:n], sem["arr%d" % j], _cols(SA), _cols(2 * j + 1)),
+                            (cores[b], out[n:], sem["arr%d" % j], _cols(SB), _cols(2 * j + 1))])
+            g.wait_ge(sem.sent, sent[0])
         return
 
     P = plan[me]
     p, a, b, c, d = P["p"], P["a"], P["b"], P["c"], P["d"]
-    out, inner = split(me)
+    out, inner = rank_split(me)
     half = len(inner) // 2
 
-    loads = _runs([a, b]) + _runs([p, c, d, me])
+    early = _runs([a, b]) + _runs([c, d])
+    loads = early + [(p, 1), (me, 1)]
     where = {}
     g.sync.dma_start(T.wt[:], T.w[:]).then_inc(sem.ldw, 16)
     queues = [g.scalar, g.sync]
     for k, (first, count) in enumerate(loads):
-        queues[k % 2].dma_start(T.xt[:, first * TB:(first + count) * TB],
-                                T.x[:, first * TB:(first + count) * TB]).then_inc(sem["ldx%d" % k], 16)
+        queue = queues[k % 2] if k < len(early) else g.sync
+        if k == len(early):
+            queue.wait_ge(sem.go, 1)
+        queue.dma_start(T.xt[:, first * TB:(first + count) * TB],
+                        T.x[:, first * TB:(first + count) * TB]).then_inc(sem["ldx%d" % k], 16)
         for t in range(first, first + count):
             where[t] = k
 
     waited = set()
 
-    def quant(tile, slot, pos, done):
-        lo, hi = _cols(slot, pos)
+    def quant(tile, place, done):
+        lo, hi = _cols(place)
         if tile is None:
-            if "w" not in waited:
-                g.vector.wait_ge(sem.ldw, 16)
-                waited.add("w")
+            g.vector.wait_ge(sem.ldw, 16)
             src = T.wt[:]
         else:
             if where[tile] not in waited:
@@ -132,55 +158,51 @@ def rank_program(g, core, T, topo):
             src = T.xt[:, tile * TB:(tile + 1) * TB]
         g.vector.quantize_mx(T.qc[:, lo:hi], T.qs[:, lo:hi], src).then_inc(done, 1)
 
-    quant(None, OWN, 1, sem.qw)
-    quant(None, me, 2, sem.qb)
+    quant(None, 2 * me, sem.qw)
     for tile in sorted([a, b], key=lambda t: where[t]):
-        quant(tile, me, {a: 1, b: 3}[tile], sem.qb)
-    for tile in sorted([p, c, d], key=lambda t: where[t]):
-        quant(tile, *{p: (me, 0), c: (OWN, 0), d: (OWN, 2)}[tile], sem.qx)
-    quant(me, OWN, 3, sem.qo)
+        quant(tile, {a: SA, b: SB}[tile], sem.qb)
+    for tile in sorted([c, d], key=lambda t: where[t]):
+        quant(tile, {c: SC, d: SD}[tile], sem.qx)
+    quant(p, SP, sem.qp)
+    quant(me, 2 * me + 1, sem.qo)
 
-    hc, hd = P["h"][c], P["h"][d]
-    w = _cols(OWN, 1)
+    hc, hd, relay = P["h"][c], P["h"][d], plan[p]["relay"]
+    w = _cols(2 * me)
     g.wait_ge(sem.qw, 1)
-    send("s", [(hc, out, sem.hw, w, w), (hd, inner, sem.hw, w, w)])
-    send("c", [(hc, inner[:half], sem.hc, w, w), (hd, inner[half:], sem.hc, w, w)])
-    g.wait_ge(sem.qb, 3)
     for kind in KINDS:
-        send(kind, [(cores[p], out, sem["arr%s%d" % (kind, me)], _cols(me, 1, 3), _cols(me, 1, 3))])
-    g.wait_ge(sem.qx, 3)
+        send(kind, [(relay, out, sem["rw" + kind], w, w),
+                    (hc, inner[:half], sem["hw" + kind], w, w),
+                    (hd, inner[half:], sem["hw" + kind], w, w)])
+    g.wait_ge(sem.qb, 2)
     for kind in KINDS:
-        send(kind, [(cores[p], out, sem["p" + kind], _cols(me, 0), _cols(me, 0)),
-                    (hc, inner[:half], sem["h" + kind], _cols(OWN, 0), _cols(OWN, 0)),
-                    (hd, inner[half:], sem["h" + kind], _cols(OWN, 2), _cols(OWN, 2))])
+        send(kind, [(relay, out, sem["rx" + kind], _cols(SA, 2), _cols(SA, 2))])
+    g.wait_ge(sem.qx, 2)
     for kind in KINDS:
-        g.wait_ge(sem["arr%s%d" % (kind, p)], len(out))
-        items = []
-        for k, r in enumerate((plan[p]["a"], plan[p]["b"])):
-            eng = _engines(topo.mask(core, cores[r]))
-            n = len(eng) // 2
-            items.append((cores[r], eng[k * n:(k + 1) * n], sem["arr%s%d" % (kind, p)], _cols(p, 1 + k, 2), _cols(p, 1 + k, 2)))
-        send(kind, items)
+        send(kind, [(hc, inner[:half], sem["hx" + kind], _cols(SC), _cols(SC)),
+                    (hd, inner[half:], sem["hx" + kind], _cols(SD), _cols(SD))])
+    g.sem_inc(sem.go, 1)
+    g.wait_ge(sem.qp, 1)
+    for kind in KINDS:
+        send(kind, [(cores[p], out, sem["arr%d" % me], _cols(SP), _cols(2 * me + 1))])
 
-    def product(w_slot, w_pos, x_slot, x_pos, first, last):
-        wl, wh = _cols(w_slot, w_pos)
-        xl, xh = _cols(x_slot, x_pos)
+    def product(j, first, last):
+        wl, wh = _cols(2 * j)
+        xl, xh = _cols(2 * j + 1)
         return g.tensor.matmul_mx(T.acc[:, 0:TW], T.qc[:, wl:wh], T.qs[:, wl:wh], T.qc[:, xl:xh], T.qs[:, xl:xh], first, last)
 
     g.tensor.wait_ge(sem.qw, 1)
     g.tensor.wait_ge(sem.qo, 1)
-    product(OWN, 1, OWN, 3, True, False)
-    order = [p, c, d, plan[c]["p"], plan[d]["p"]]
+    product(me, True, False)
+    order = [plan[c]["p"], plan[d]["p"], c, d, p]
     for k, j in enumerate(order):
-        Q = plan[j]
-        near = me in (Q["c"], Q["d"])
-        for letter in KINDS + (("w",) if near else ()):
-            g.tensor.wait_ge(sem["arr%s%d" % (letter, j)], len(out) if (near or me == Q["p"]) else len(out) // 2)
-        if me == Q["p"]:
-            for kind in KINDS:
-                g.tensor.wait_ge(sem["p" + kind], len(out))
-        pos = 0 if me == Q["p"] else (1 if me in (Q["a"], Q["c"]) else 3)
-        ins = product(j, 2, j, pos, False, k == len(order) - 1)
+        if j == p:
+            total = 2 * len(relay_split(me)[1]) + 2 * len(rank_split(j)[0])
+        elif j in (c, d):
+            total = 4 * len(_engines(topo.mask(plan[j]["h"][me], core)))
+        else:
+            total = 4 * (len(relay_split(plan[j]["p"])[0]) // 2)
+        g.tensor.wait_ge(sem["arr%d" % j], total)
+        ins = product(j, False, k == len(order) - 1)
     ins.then_inc(sem.mm, 1)
 
     g.vector.wait_ge(sem.mm, 1)

from concourse.bass import DstId, RemoteDMATransfer
from concourse.mybir import dt

N = 6
TW = 128
TB = 4 * TW
SA, SB, SP, SC, SD = (2 * N + k for k in range(5))
TILES = 2 * N + 5
KINDS = ("s", "c")

SCRATCH = {
    "wt": ("sbuf", [128, TB], "bfloat16"),
    "xt": ("sbuf", [128, N * TB], "bfloat16"),
    "qc": ("sbuf", [128, TILES * TW], "float8_e4m3fn_x4"),
    "qs": ("sbuf", [128, TILES * TW], "uint8"),
    "acc": ("psum", [128, 512], "float32"),
    "yt": ("sbuf", [128, TW], "float32"),
}
SEMAPHORES = (["ldw"] + ["ldx%d" % k for k in range(N)] + ["qw", "qb", "qx", "qp", "qo", "go", "sent", "mm", "cp", "st"]
              + [a + b + k for a in "hr" for b in "wx" for k in KINDS] + ["arr%d" % j for j in range(N)])


def _plan(cores, topo):
    plan = []
    for j, cj in enumerate(cores):
        rack = topo.rack(topo.host(cj))
        near = [r for r, c in enumerate(cores) if r != j and topo.rack(topo.host(c)) == rack]
        far = [r for r, c in enumerate(cores) if topo.rack(topo.host(c)) != rack]
        p = [r for r in far if topo.may_write(cj, cores[r]) and topo.chip(cores[r]) == topo.chip(cj)][0]
        a, b = [r for r in far if r != p]
        chip = [h for h in range(topo.host(cj) * topo.CORES_PER_HOST, (topo.host(cj) + 1) * topo.CORES_PER_HOST)
                if topo.chip(h) == topo.chip(cj) and h not in cores]
        other = [h for h in chip if topo.die(h) != topo.die(cj)]
        fit = {r: [h for h in other if topo.may_write(h, cores[r])] for r in near}
        helper = {}
        for r in sorted(near, key=lambda r: len(fit[r])):
            helper[r] = [h for h in fit[r] if h not in helper.values()][-1]
        relay = [h for h in chip if topo.die(h) == topo.die(cj) and all(topo.may_write(h, cores[r]) for r in near)][-1]
        plan.append({"p": p, "a": a, "b": b, "c": near[0], "d": near[1], "h": helper, "relay": relay})
    return plan


def _runs(tiles):
    out = []
    for t in sorted(tiles):
        if out and out[-1][0] + out[-1][1] == t:
            out[-1] = (out[-1][0], out[-1][1] + 1)
        else:
            out.append((t, 1))
    return out


def _engines(mask):
    return [1 << k for k in range(16) if mask >> k & 1]


def _join(bits):
    m = 0
    for b in bits:
        m |= b
    return m


def _cols(tile, tiles=1):
    return tile * TW, (tile + tiles) * TW


def rank_program(g, core, T, topo):
    cores = list(T.cores)
    plan = _plan(cores, topo)
    sem = T.sem
    sent = [0]

    def view(kind, lo, hi):
        return T.qc[:, lo:hi].bitcast(dt.uint8) if kind == "c" else T.qs[:, lo:hi]

    def send(kind, items):
        trs = []
        for dst, eng, rsem, s, t in items:
            rid, pid = topo.addr(dst, core)
            trs.append(RemoteDMATransfer(dst_ids=[DstId(rid=rid, pnc=pid)], dma_engine_mask=_join(eng), remote_sem=rsem,
                                         src=view(kind, *s), dst=view(kind, *t)))
            sent[0] += len(eng)
        g.remote_dma_fused(trs, local_sem=sem.sent)

    def split(src, off, on):
        out = _engines(topo.mask(src, off))
        return out, [e for e in _engines(topo.mask(src, on)) if e not in out]

    def rank_split(j):
        return split(cores[j], plan[plan[j]["p"]]["relay"], plan[j]["h"][plan[j]["c"]])

    def relay_split(q):
        return split(plan[q]["relay"], cores[plan[q]["c"]], cores[q])

    me = T.rank_of(core)
    if me is None:
        for j in range(N):
            for k, r in enumerate((plan[j]["c"], plan[j]["d"])):
                if plan[j]["h"][r] != core:
                    continue
                count = len(rank_split(j)[1]) // 2
                eng = _engines(topo.mask(core, cores[r]))
                for what, src, dst in (("w", 2 * j, 2 * j), ("x", SC + k, 2 * j + 1)):
                    for kind in KINDS:
                        g.wait_ge(sem["h" + what + kind], count)
                        send(kind, [(cores[r], eng, sem["arr%d" % j], _cols(src), _cols(dst))])
                g.wait_ge(sem.sent, sent[0])
            q = plan[j]["p"]
            if plan[q]["relay"] != core:
                continue
            count = len(rank_split(j)[0])
            out, inner = relay_split(q)
            n = len(out) // 2
            a, b = plan[j]["a"], plan[j]["b"]
            for kind in KINDS:
                g.wait_ge(sem["rw" + kind], count)
                send(kind, [(cores[a], out[:n], sem["arr%d" % j], _cols(2 * j), _cols(2 * j)),
                            (cores[b], out[n:], sem["arr%d" % j], _cols(2 * j), _cols(2 * j)),
                            (cores[q], inner, sem["arr%d" % j], _cols(2 * j), _cols(2 * j))])
            for kind in KINDS:
                g.wait_ge(sem["rx" + kind], count)
                send(kind, [(cores[a], out[:n], sem["arr%d" % j], _cols(SA), _cols(2 * j + 1)),
                            (cores[b], out[n:], sem["arr%d" % j], _cols(SB), _cols(2 * j + 1))])
            g.wait_ge(sem.sent, sent[0])
        return

    P = plan[me]
    p, a, b, c, d = P["p"], P["a"], P["b"], P["c"], P["d"]
    out, inner = rank_split(me)
    half = len(inner) // 2

    early = _runs([a, b]) + _runs([c, d])
    loads = early + [(p, 1), (me, 1)]
    where = {}
    g.sync.dma_start(T.wt[:], T.w[:]).then_inc(sem.ldw, 16)
    queues = [g.scalar, g.sync]
    for k, (first, count) in enumerate(loads):
        queue = queues[k % 2] if k < len(early) else g.sync
        if k == len(early):
            queue.wait_ge(sem.go, 1)
        queue.dma_start(T.xt[:, first * TB:(first + count) * TB],
                        T.x[:, first * TB:(first + count) * TB]).then_inc(sem["ldx%d" % k], 16)
        for t in range(first, first + count):
            where[t] = k

    waited = set()

    def quant(tile, place, done):
        lo, hi = _cols(place)
        if tile is None:
            g.vector.wait_ge(sem.ldw, 16)
            src = T.wt[:]
        else:
            if where[tile] not in waited:
                g.vector.wait_ge(sem["ldx%d" % where[tile]], 16)
                waited.add(where[tile])
            src = T.xt[:, tile * TB:(tile + 1) * TB]
        g.vector.quantize_mx(T.qc[:, lo:hi], T.qs[:, lo:hi], src).then_inc(done, 1)

    quant(None, 2 * me, sem.qw)
    for tile in sorted([a, b], key=lambda t: where[t]):
        quant(tile, {a: SA, b: SB}[tile], sem.qb)
    for tile in sorted([c, d], key=lambda t: where[t]):
        quant(tile, {c: SC, d: SD}[tile], sem.qx)
    quant(p, SP, sem.qp)
    quant(me, 2 * me + 1, sem.qo)

    hc, hd, relay = P["h"][c], P["h"][d], plan[p]["relay"]
    w = _cols(2 * me)
    g.wait_ge(sem.qw, 1)
    for kind in KINDS:
        send(kind, [(relay, out, sem["rw" + kind], w, w),
                    (hc, inner[:half], sem["hw" + kind], w, w),
                    (hd, inner[half:], sem["hw" + kind], w, w)])
    g.wait_ge(sem.qb, 2)
    for kind in KINDS:
        send(kind, [(relay, out, sem["rx" + kind], _cols(SA, 2), _cols(SA, 2))])
    g.wait_ge(sem.qx, 2)
    for kind in KINDS:
        send(kind, [(hc, inner[:half], sem["hx" + kind], _cols(SC), _cols(SC)),
                    (hd, inner[half:], sem["hx" + kind], _cols(SD), _cols(SD))])
    g.sem_inc(sem.go, 1)
    g.wait_ge(sem.qp, 1)
    for kind in KINDS:
        send(kind, [(cores[p], out, sem["arr%d" % me], _cols(SP), _cols(2 * me + 1))])

    def product(j, first, last):
        wl, wh = _cols(2 * j)
        xl, xh = _cols(2 * j + 1)
        return g.tensor.matmul_mx(T.acc[:, 0:TW], T.qc[:, wl:wh], T.qs[:, wl:wh], T.qc[:, xl:xh], T.qs[:, xl:xh], first, last)

    g.tensor.wait_ge(sem.qw, 1)
    g.tensor.wait_ge(sem.qo, 1)
    product(me, True, False)
    order = [plan[c]["p"], plan[d]["p"], c, d, p]
    for k, j in enumerate(order):
        if j == p:
            total = 2 * len(relay_split(me)[1]) + 2 * len(rank_split(j)[0])
        elif j in (c, d):
            total = 4 * len(_engines(topo.mask(plan[j]["h"][me], core)))
        else:
            total = 4 * (len(relay_split(plan[j]["p"])[0]) // 2)
        g.tensor.wait_ge(sem["arr%d" % j], total)
        ins = product(j, False, k == len(order) - 1)
    ins.then_inc(sem.mm, 1)

    g.vector.wait_ge(sem.mm, 1)
    g.vector.tensor_copy(T.yt[:], T.acc[:, 0:TW]).then_inc(sem.cp, 1)
    g.sync.wait_ge(sem.cp, 1)
    g.sync.dma_start(T.y[:], T.yt[:]).then_inc(sem.st, 16)
    g.sync.wait_ge(sem.st, 16)
    g.wait_ge(sem.sent, sent[0])
